import numpy as np
import ml_dtypes


def mxq(x, axis, fmt="e4m3"):
    dtype, down = {"e4m3": (ml_dtypes.float8_e4m3fn, 7), "e5m2": (ml_dtypes.float8_e5m2, 14)}[fmt]
    v = np.moveaxis(np.asarray(x, np.float32).astype(ml_dtypes.bfloat16).astype(np.float64), axis, -1)
    blocks = v.reshape(v.shape[:-1] + (-1, 32))
    amax = np.abs(blocks).max(-1, keepdims=True)
    byte = np.maximum(np.where(amax > 0, np.frexp(amax)[1] - 1 + 127, 0) - down, 1)
    scale = np.exp2(byte - 127.0)
    codes = (blocks / scale).astype(np.float32).astype(dtype).astype(np.float64)
    return np.moveaxis((codes * scale).reshape(v.shape), -1, axis)


WIDE = False


def mx_kscale(k):
    if not WIDE:
        return np.ones(k)
    levels = np.array([30, -30])
    if k % 512:
        return np.exp2(np.random.permutation(np.resize(levels, k // 32))).repeat(32)
    a = np.empty((k // 512, 16))
    for p in range(k // 512):
        a[p, :8] = np.random.permutation(np.resize(levels, 8))
        for g in range(8):
            far = levels[np.abs(levels - a[p, g]) >= 10]
            a[p, g + 8] = far[np.random.randint(len(far))]
    return np.exp2(a.ravel()).repeat(32)


def f64(x):
    return np.asarray(x).astype(np.float64)


def striped(idx):
    return np.tile(np.asarray(idx).reshape(-1, 16).T, (8, 1)).astype(np.uint16)


def unstriped(offs):
    return offs[:16].T.reshape(-1).astype(np.int64)


E2M1 = np.array([0.0, 0.5, 1.0, 1.5, 2.0, 3.0, 4.0, 6.0, -0.0, -0.5, -1.0, -1.5, -2.0, -3.0, -4.0, -6.0])


def pack_weight(w, fmt):
    k, n = w.shape
    w = f64(np.asarray(w, np.float32).astype(ml_dtypes.bfloat16)).reshape(k // 32, 32, n)
    amax = np.abs(w).max(1)
    if fmt in ("e4m3", "e5m2"):
        byte = np.frexp(amax)[1] - 1 + 127 - (7 if fmt == "e4m3" else 14)
    else:
        mant, ex = np.frexp(amax / 6.0)
        byte = np.where(mant > 0.5, ex, ex - 1) + 127
    byte = np.clip(np.where(amax > 0, byte, 1), 1, 254)
    scaled = (w * np.exp2(127.0 - byte)[:, None, :]).reshape(k, n).astype(np.float32)
    by_word = np.ascontiguousarray(scaled.reshape(k // 512, 128, 4, n).transpose(0, 1, 3, 2))
    if fmt in ("e4m3", "e5m2"):
        words = by_word.astype(ml_dtypes.float8_e4m3fn if fmt == "e4m3" else ml_dtypes.float8_e5m2).view(np.uint8)
    else:
        c = by_word.astype(ml_dtypes.float4_e2m1fn).view(np.uint8) & 0xF
        words = (c[..., 0::2] | (c[..., 1::2] << 4)).reshape(k // 512, 128, 2 * n)
    return np.ascontiguousarray(words), np.ascontiguousarray(byte.astype(np.uint8).reshape(k // 512, 16, n))


def unpack_weight(words, scales, fmt):
    g, _, n = scales.shape
    words = np.ascontiguousarray(words).reshape(g, 128, n, -1)
    if fmt in ("e4m3", "e5m2"):
        vals = words.view(ml_dtypes.float8_e4m3fn if fmt == "e4m3" else ml_dtypes.float8_e5m2).astype(np.float64)
    else:
        nib = np.empty((g, 128, n, 4), np.uint8)
        nib[..., 0::2] = words & 0xF
        nib[..., 1::2] = words >> 4
        vals = E2M1[nib]
    vals = vals * np.repeat(np.exp2(scales.astype(np.float64) - 127.0), 8, axis=1)[..., None]
    return vals.transpose(0, 1, 3, 2).reshape(g * 512, n)


def sigmoid(v):
    return 1.0 / (1.0 + np.exp(-v))


K, T, Z, J, R, Q, N, L, E = 512, 1024, 1024, 256, 512, 1024, 256, 512, 1024


def setup_inputs():
    n = np.random.standard_normal
    idx = np.random.permutation(T)[:J]
    idx2 = np.random.permutation(Z)[:J]
    idx3 = np.random.permutation(Q)[:J]
    idx4 = np.random.permutation(E)[:J]
    fk = mx_kscale(K)
    fr = mx_kscale(R)
    fl = mx_kscale(L)
    xtp = pack_weight(n((K, T)) / fk[:, None], "e2m1")
    xop = pack_weight(n((K, Z)) / fk[:, None], "e5m2")
    wp = pack_weight(n((K, R)) * 1 / np.sqrt(K) * fk[:, None] * fr, "e5m2")
    w2p = pack_weight(n((K, R)) * 1 / np.sqrt(K) * fk[:, None] * fr, "e4m3")
    wbp = pack_weight(n((R, N)) * 1 / np.sqrt(R) / fr[:, None], "e4m3")
    sxp = pack_weight(n((L, J)) / fl[:, None], "e5m2")
    wsp = pack_weight(n((L, N)) * 1 / np.sqrt(L) * fl[:, None], "e4m3")
    return {
        "xt_words": xtp[0],
        "xt_scales": xtp[1],
        "xo_words": xop[0],
        "xo_scales": xop[1],
        "w_words": wp[0],
        "w_scales": wp[1],
        "w2_words": w2p[0],
        "w2_scales": w2p[1],
        "tg": (1.0 * n((R, Q))).astype(np.float32),
        "sg": (np.random.uniform(0.6, 1.6, (R, 1))).astype(np.float32),
        "bg": (np.random.uniform(-1.0, 1.0, (R, 1))).astype(np.float32),
        "wb_words": wbp[0],
        "wb_scales": wbp[1],
        "sx_words": sxp[0],
        "sx_scales": sxp[1],
        "ws_words": wsp[0],
        "ws_scales": wsp[1],
        "offs": striped(idx),
        "offs2": striped(idx2),
        "offs3": striped(idx3),
        "offs4": striped(idx4),
    }


def reference(xt_words, xt_scales, xo_words, xo_scales, w_words, w_scales, w2_words, w2_scales, tg, sg, bg, wb_words, wb_scales, sx_words, sx_scales, ws_words, ws_scales, offs, offs2, offs3, offs4):
    idx = unstriped(offs)
    idx2 = unstriped(offs2)
    idx3 = unstriped(offs3)
    idx4 = unstriped(offs4)
    xtu = unpack_weight(xt_words, xt_scales, "e2m1")
    xou = unpack_weight(xo_words, xo_scales, "e5m2")
    wu = unpack_weight(w_words, w_scales, "e5m2")
    w2u = unpack_weight(w2_words, w2_scales, "e4m3")
    wbu = unpack_weight(wb_words, wb_scales, "e4m3")
    sxu = unpack_weight(sx_words, sx_scales, "e5m2")
    wsu = unpack_weight(ws_words, ws_scales, "e4m3")
    xtidxg = xtu[:, idx]
    xoidx2g = xou[:, idx2]
    a = wu.T @ xtidxg + w2u.T @ xoidx2g
    b = w2u.T @ xtidxg + wu.T @ xoidx2g
    hid = np.abs(a - b) * sigmoid(f64(tg)[:, idx3] * f64(sg) + f64(bg))
    hidq = mxq(hid, 0, "e5m2")
    p = wbu.T @ hidq + wsu.T @ sxu
    y = np.zeros((N, E))
    y[:, idx4] = p
    return y

@@ -1,0 +1,214 @@
+from contextlib import ExitStack
+
+import concourse.mybir as mybir
+
+K, T, J, R, N, E = 512, 1024, 256, 512, 256, 1024
+FLOPS = 2 * (4 * K * R * J + R * N * J + K * N * J)
+
+F32 = mybir.dt.float32
+BF16 = mybir.dt.bfloat16
+I32 = mybir.dt.int32
+U32 = mybir.dt.uint32
+U16 = mybir.dt.uint16
+U8 = mybir.dt.uint8
+E4M3 = mybir.dt.float8_e4m3fn_x4
+E5M2 = mybir.dt.float8_e5m2_x4
+E2M1 = mybir.dt.float4_e2m1fn_x4
+ACT = mybir.ActivationFunctionType
+ALU = mybir.AluOpType
+
+P = 128
+PACK = 4
+SCALE_ROWS = 16
+HALF = 128
+HALVES = J // HALF
+PIECES = 2
+RUN = 4
+RUNS = HALF // (PIECES * RUN)
+
+
+def words_of(ap):
+    return ap[0].rearrange("p c b -> p (c b)").bitcast(I32)
+
+
+def tile_list_crossed_tablegate_skip_scattered_kernel(
+    tc, xt_words, xt_scales, xo_words, xo_scales, w_words, w_scales, w2_words, w2_scales, tg, sg, bg,
+    wb_words, wb_scales, sx_words, sx_scales, ws_words, ws_scales, offs, offs2, offs3, offs4, out,
+):
+    nc = tc.nc
+    with ExitStack() as ctx:
+        pool = ctx.enter_context(tc.tile_pool(name="pool", bufs=1))
+        psum = ctx.enter_context(tc.psum_pool(name="psum", bufs=1))
+
+        def tile(shape, dtype, name, tag=None):
+            return pool.tile(shape, dtype, name=name, tag=tag or name, align_bytes=64)
+
+        def load_scale_rows(queue, dst, src):
+            queue.dma_start(out=dst[0:SCALE_ROWS, :].bitcast(I32), in_=src[0].bitcast(I32))
+
+        def spread_scale_rows(queue, plane):
+            for q in range(1, 4):
+                queue.dma_start(out=plane[32 * q : 32 * q + 4, :].bitcast(I32), in_=plane[4 * q : 4 * q + 4, :].bitcast(I32))
+
+        list_t = tile([P, J // 16], U16, "list_t")
+        list_o = tile([P, J // 16], U16, "list_o")
+        list_g = tile([P, J // 16], U16, "list_g")
+        list_p = tile([P, J // 16], U16, "list_p")
+
+        xt_rows = tile([P, T], U8, "xt_rows")
+        xo_rows = tile([P, T], U8, "xo_rows")
+        w_rows = tile([P, 2 * R], U8, "w_rows")
+        late_plane = tile([P, 2 * N + J], U8, "late_plane")
+        nc.gpsimd.memset(xt_rows[:].bitcast(I32), 0)
+        nc.gpsimd.memset(xo_rows[:].bitcast(I32), 0)
+        nc.vector.memset(w_rows[:].bitcast(I32), 0)
+        nc.gpsimd.memset(late_plane[:].bitcast(I32), 0)
+
+        xt_table = tile([P, T], U16, "xt_table")
+        xo_table = tile([P, T], U32, "xo_table")
+        w_raw = tile([P, R], I32, "w_raw")
+        w2_raw = tile([P, R], I32, "w2_raw")
+        gates = [tile([P, T], F32, "gates%d" % t) for t in range(PACK)]
+        slope = tile([P, PACK], F32, "slope")
+        shift = tile([P, PACK], F32, "shift")
+
+        nc.sync.dma_start(list_t[:], offs)
+        nc.sync.dma_start(list_o[:], offs2)
+        load_scale_rows(nc.scalar, xt_rows, xt_scales)
+        load_scale_rows(nc.scalar, xo_rows, xo_scales)
+        load_scale_rows(nc.scalar, w_rows[:, 0:R], w_scales)
+        load_scale_rows(nc.scalar, w_rows[:, R : 2 * R], w2_scales)
+        nc.sync.dma_start(out=xt_table[:].bitcast(I32), in_=xt_words[0].bitcast(I32))
+        nc.sync.dma_start(out=xo_table[:].bitcast(I32), in_=words_of(xo_words))
+        nc.sync.dma_start(out=w2_raw[:], in_=words_of(w2_words))
+        nc.sync.dma_start(out=w_raw[:], in_=words_of(w_words))
+        nc.sync.dma_start(list_g[:], offs3)
+        tg_dealt = tg.rearrange("(p t) q -> p t q", t=PACK)
+        for t in range(PACK):
+            nc.sync.dma_start(out=gates[t][:], in_=tg_dealt[:, t, :])
+        nc.sync.dma_start(list_p[:], offs4)
+
+        wb_cols, sx_cols, ws_cols = slice(0, N), slice(N, N + J), slice(N + J, 2 * N + J)
+        load_scale_rows(nc.gpsimd, late_plane[:, wb_cols], wb_scales)
+        load_scale_rows(nc.gpsimd, late_plane[:, sx_cols], sx_scales)
+        load_scale_rows(nc.gpsimd, late_plane[:, ws_cols], ws_scales)
+        nc.gpsimd.dma_start(out=slope[:], in_=sg.rearrange("(p t) o -> p (t o)", t=PACK))
+        nc.gpsimd.dma_start(out=shift[:], in_=bg.rearrange("(p t) o -> p (t o)", t=PACK))
+        spread_scale_rows(nc.gpsimd, late_plane)
+
+        pages = [tile([P, E], F32, "page%d" % nt) for nt in range(N // P)]
+        for page in pages:
+            nc.vector.memset(page[:], 0.0)
+
+        xt_picked_rows = tile([P, J], U8, "xt_picked_rows")
+        xo_picked_rows = tile([P, J], U8, "xo_picked_rows")
+        plane = tile([P, 2 * J + 2 * R], U8, "plane")
+        nc.vector.tensor_copy(xt_picked_rows[:], xt_rows[:].indirect(list_t[:]))
+        nc.vector.tensor_copy(xo_picked_rows[:], xo_rows[:].indirect(list_o[:]))
+        nc.vector.tensor_copy(
+            plane[:, 2 * J :].rearrange("p (w t m) -> p w m t", w=2, t=PACK),
+            w_rows[:].rearrange("p (w m t) -> p w m t", w=2, t=PACK),
+        )
+        nc.vector.tensor_copy(plane[:, 0:J].bitcast(I32), xt_picked_rows[:].bitcast(I32))
+        nc.vector.tensor_copy(plane[:, J : 2 * J].bitcast(I32), xo_picked_rows[:].bitcast(I32))
+        spread_scale_rows(nc.scalar, plane)
+
+        xt_picked = tile([P, J], U16, "xt_picked")
+        xo_picked = tile([P, J], U32, "xo_picked")
+        w_dealt = tile([P, R], I32, "w_dealt")
+        w2_dealt = tile([P, R], I32, "w2_dealt")
+        nc.vector.tensor_copy(xt_picked[:], xt_table[:].indirect(list_t[:]))
+        nc.vector.tensor_copy(xo_picked[:], xo_table[:].indirect(list_o[:]))
+        for dealt, raw in ((w2_dealt, w2_raw), (w_dealt, w_raw)):
+            nc.vector.tensor_copy(
+                dealt[:].rearrange("p (t m) -> p m t", t=PACK), raw[:].rearrange("p (m t) -> p m t", t=PACK)
+            )
+
+        sx_sb = tile([P, J], U32, "sx_sb", tag="xo_table")
+        ws_sb = tile([P, N], U32, "ws_sb", tag="w2_raw")
+        wb_sb = tile([P, N], U32, "wb_sb", tag="w_raw")
+        nc.sync.dma_start(out=sx_sb[:].bitcast(I32), in_=words_of(sx_words))
+        nc.sync.dma_start(out=ws_sb[:].bitcast(I32), in_=words_of(ws_words))
+        nc.sync.dma_start(out=wb_sb[:].bitcast(I32), in_=words_of(wb_words))
+
+        gate = tile([P, PACK, J], F32, "gate")
+        for t in range(PACK):
+            nc.scalar.activation(
+                out=gate[:, t, :], in_=gates[t][:].indirect(list_g[:]), func=ACT.Sigmoid,
+                bias=shift[:, t : t + 1], scale=slope[:, t : t + 1],
+            )
+
+        def first_stage(acc, h, with_xt, with_xo):
+            cols = slice(h * HALF, (h + 1) * HALF)
+            moving = (
+                (with_xt, xt_picked[:, cols].bitcast(E2M1), plane[:, h * HALF : (h + 1) * HALF]),
+                (with_xo, xo_picked[:, cols].bitcast(E5M2), plane[:, J + h * HALF : J + (h + 1) * HALF]),
+            )
+            for t in range(PACK):
+                for n, ((dealt, fmt, first_col), rhs, rhs_scale) in enumerate(moving):
+                    nc.tensor.matmul_mx(
+                        out=acc[:, t, :],
+                        lhsT=dealt[:, t * P : (t + 1) * P].bitcast(fmt),
+                        lhsT_scale=plane[:, first_col + t * P : first_col + (t + 1) * P],
+                        rhs=rhs, rhs_scale=rhs_scale, start=(n == 0), stop=(n == 1),
+                    )
+
+        w_side = (w_dealt, E5M2, 2 * J)
+        w2_side = (w2_dealt, E4M3, 2 * J + R)
+        acc_a = [psum.tile([P, PACK, HALF], F32, name="acc_a%d" % h, tag="bank_a%d" % h) for h in range(HALVES)]
+        acc_b = [psum.tile([P, PACK, HALF], F32, name="acc_b%d" % h, tag="bank_b%d" % h) for h in range(HALVES)]
+        for h in range(HALVES):
+            first_stage(acc_b[h], h, w2_side, w_side)
+            first_stage(acc_a[h], h, w_side, w2_side)
+
+
+        def by_runs(ap, first):
+            return ap[:, :, first : first + RUNS * RUN].rearrange("p t (c i) -> p c t i", i=RUN)
+
+        for h in range(HALVES):
+            b_sb = [tile([P, RUNS, PACK, RUN], F32, "b_sb%d_%d" % (h, s)) for s in range(PIECES)]
+            diff = [tile([P, RUNS, PACK, RUN], F32, "diff%d_%d" % (h, s)) for s in range(PIECES)]
+            size = [tile([P, RUNS, PACK, RUN], F32, "size%d_%d" % (h, s)) for s in range(PIECES)]
+            hid = tile([P, PIECES, RUNS, RUN, PACK], BF16, "hid%d" % h)
+            for s in range(PIECES):
+                nc.scalar.copy(out=b_sb[s][:], in_=by_runs(acc_b[h], s * RUNS * RUN))
+            for s in range(PIECES):
+                nc.vector.tensor_tensor(out=diff[s][:], in0=by_runs(acc_a[h], s * RUNS * RUN), in1=b_sb[s][:], op=ALU.subtract)
+                nc.scalar.activation(out=size[s][:], in_=diff[s][:], func=ACT.Abs)
+            acc_p = [psum.tile([P, HALF], F32, name="acc_p%d_%d" % (h, nt), tag="bank_%s%d" % (side, h)) for nt, side in enumerate("ba")]
+            for nt in range(N // P):
+                nc.tensor.matmul_mx(
+                    out=acc_p[nt][:],
+                    lhsT=ws_sb[:, nt * P : (nt + 1) * P].bitcast(E4M3),
+                    lhsT_scale=late_plane[:, N + J + nt * P : N + J + (nt + 1) * P],
+                    rhs=sx_sb[:, h * HALF : (h + 1) * HALF].bitcast(E5M2),
+                    rhs_scale=late_plane[:, N + h * HALF : N + (h + 1) * HALF],
+                    start=True, stop=False,
+                )
+            for s in range(PIECES):
+                nc.vector.tensor_tensor(
+                    out=hid[:, s].rearrange("p c i t -> p c t i"), in0=size[s][:],
+                    in1=by_runs(gate, h * HALF + s * RUNS * RUN), op=ALU.mult,
+                )
+            hid_words = tile([P, HALF], U32, "hid_words%d" % h)
+            hid_plane = tile([P, HALF], U8, "hid_plane%d" % h)
+            nc.vector.quantize_mx(
+                out=hid_words[:].bitcast(E5M2), scales=hid_plane[:], in_=hid[:].rearrange("p s c i t -> p (s c i t)")
+            )
+            places = list_p[:, h * HALF // 16 : (h + 1) * HALF // 16]
+            for nt in range(N // P):
+                nc.tensor.matmul_mx(
+                    out=acc_p[nt][:],
+                    lhsT=wb_sb[:, nt * P : (nt + 1) * P].bitcast(E4M3),
+                    lhsT_scale=late_plane[:, nt * P : (nt + 1) * P],
+                    rhs=hid_words[:].bitcast(E5M2), rhs_scale=hid_plane[:],
+                    start=False, stop=True,
+                )
+            p_sb = [tile([P, HALF], F32, "p_sb%d_%d" % (h, nt)) for nt in range(N // P)]
+            nc.vector.tensor_copy(p_sb[0][:], acc_p[0][:])
+            nc.scalar.copy(out=p_sb[1][:], in_=acc_p[1][:])
+            nc.vector.tensor_copy(pages[0][:].indirect(places), p_sb[0][:])
+            nc.scalar.activation(out=pages[1][:].indirect(places), in_=p_sb[1][:], func=ACT.Copy)
+
+        nc.sync.dma_start(out=out[0:P, :], in_=pages[0][:])
+        nc.scalar.dma_start(out=out[P : 2 * P, :], in_=pages[1][:])

@@ -58,11 +58,12 @@ def tile_list_crossed_tablegate_skip_scattered_kernel(
         xt_rows = tile([P, T], U8, "xt_rows")
         xo_rows = tile([P, T], U8, "xo_rows")
         w_rows = tile([P, 2 * R], U8, "w_rows")
-        late_plane = tile([P, 2 * N + J], U8, "late_plane")
+        plane = tile([P, 2 * J + 2 * R + 2 * N + J], U8, "plane")
+        late_plane = plane[:, 2 * J + 2 * R :]
         nc.gpsimd.memset(xt_rows[:].bitcast(I32), 0)
         nc.gpsimd.memset(xo_rows[:].bitcast(I32), 0)
         nc.vector.memset(w_rows[:].bitcast(I32), 0)
-        nc.gpsimd.memset(late_plane[:].bitcast(I32), 0)
+        nc.vector.memset(late_plane.bitcast(I32), 0)
 
         xt_table = tile([P, T], U16, "xt_table")
         xo_table = tile([P, T], U32, "xo_table")
@@ -72,64 +73,67 @@ def tile_list_crossed_tablegate_skip_scattered_kernel(
         slope = tile([P, PACK], F32, "slope")
         shift = tile([P, PACK], F32, "shift")
 
+        wb_sb = tile([P, N], U32, "wb_sb")
+        sx_sb = tile([P, J], U32, "sx_sb")
+        ws_sb = tile([P, N], U32, "ws_sb")
+        wb_cols, sx_cols, ws_cols = slice(0, N), slice(N, N + J), slice(N + J, 2 * N + J)
+        tg_dealt = tg.rearrange("(p t) q -> p t q", t=PACK)
+
         nc.sync.dma_start(list_t[:], offs)
         nc.sync.dma_start(list_o[:], offs2)
-        load_scale_rows(nc.scalar, xt_rows, xt_scales)
-        load_scale_rows(nc.scalar, xo_rows, xo_scales)
+        load_scale_rows(nc.sync, xt_rows, xt_scales)
+        load_scale_rows(nc.sync, xo_rows, xo_scales)
         load_scale_rows(nc.scalar, w_rows[:, 0:R], w_scales)
         load_scale_rows(nc.scalar, w_rows[:, R : 2 * R], w2_scales)
         nc.sync.dma_start(out=xt_table[:].bitcast(I32), in_=xt_words[0].bitcast(I32))
         nc.sync.dma_start(out=xo_table[:].bitcast(I32), in_=words_of(xo_words))
+        load_scale_rows(nc.sync, late_plane[:, wb_cols], wb_scales)
+        load_scale_rows(nc.sync, late_plane[:, sx_cols], sx_scales)
+        load_scale_rows(nc.sync, late_plane[:, ws_cols], ws_scales)
         nc.sync.dma_start(out=w2_raw[:], in_=words_of(w2_words))
         nc.sync.dma_start(out=w_raw[:], in_=words_of(w_words))
         nc.sync.dma_start(list_g[:], offs3)
-        tg_dealt = tg.rearrange("(p t) q -> p t q", t=PACK)
-        for t in range(PACK):
-            nc.sync.dma_start(out=gates[t][:], in_=tg_dealt[:, t, :])
-        nc.sync.dma_start(list_p[:], offs4)
+        nc.sync.dma_start(out=gates[0][:], in_=tg_dealt[:, 0, :])
+        nc.sync.dma_start(out=slope[:], in_=sg.rearrange("(p t) o -> p (t o)", t=PACK))
 
-        wb_cols, sx_cols, ws_cols = slice(0, N), slice(N, N + J), slice(N + J, 2 * N + J)
-        load_scale_rows(nc.gpsimd, late_plane[:, wb_cols], wb_scales)
-        load_scale_rows(nc.gpsimd, late_plane[:, sx_cols], sx_scales)
-        load_scale_rows(nc.gpsimd, late_plane[:, ws_cols], ws_scales)
-        nc.gpsimd.dma_start(out=slope[:], in_=sg.rearrange("(p t) o -> p (t o)", t=PACK))
-        nc.gpsimd.dma_start(out=shift[:], in_=bg.rearrange("(p t) o -> p (t o)", t=PACK))
-        spread_scale_rows(nc.gpsimd, late_plane)
+        warm_in = tile([P, 1], F32, "warm_in")
+        warm_out = tile([P, 1], F32, "warm_out")
+        nc.gpsimd.memset(warm_in[:], 0.0)
+        nc.scalar.activation(out=warm_out[:], in_=warm_in[:], func=ACT.Sigmoid)
 
         pages = [tile([P, E], F32, "page%d" % nt) for nt in range(N // P)]
-        for page in pages:
-            nc.vector.memset(page[:], 0.0)
+        nc.vector.memset(pages[0][:], 0.0)
+        nc.gpsimd.memset(pages[1][:], 0.0)
 
         xt_picked_rows = tile([P, J], U8, "xt_picked_rows")
         xo_picked_rows = tile([P, J], U8, "xo_picked_rows")
-        plane = tile([P, 2 * J + 2 * R], U8, "plane")
         nc.vector.tensor_copy(xt_picked_rows[:], xt_rows[:].indirect(list_t[:]))
         nc.vector.tensor_copy(xo_picked_rows[:], xo_rows[:].indirect(list_o[:]))
         nc.vector.tensor_copy(
-            plane[:, 2 * J :].rearrange("p (w t m) -> p w m t", w=2, t=PACK),
+            plane[:, 2 * J : 2 * J + 2 * R].rearrange("p (w t m) -> p w m t", w=2, t=PACK),
             w_rows[:].rearrange("p (w m t) -> p w m t", w=2, t=PACK),
         )
         nc.vector.tensor_copy(plane[:, 0:J].bitcast(I32), xt_picked_rows[:].bitcast(I32))
         nc.vector.tensor_copy(plane[:, J : 2 * J].bitcast(I32), xo_picked_rows[:].bitcast(I32))
-        spread_scale_rows(nc.scalar, plane)
+        spread_scale_rows(nc.sync, plane)
+        nc.sync.dma_start(out=shift[:], in_=bg.rearrange("(p t) o -> p (t o)", t=PACK))
+        for t in range(1, PACK):
+            nc.sync.dma_start(out=gates[t][:], in_=tg_dealt[:, t, :])
+        nc.sync.dma_start(out=sx_sb[:].bitcast(I32), in_=words_of(sx_words))
+        nc.sync.dma_start(out=ws_sb[:].bitcast(I32), in_=words_of(ws_words))
+        nc.sync.dma_start(out=wb_sb[:].bitcast(I32), in_=words_of(wb_words))
+        nc.sync.dma_start(list_p[:], offs4)
 
-        xt_picked = tile([P, J], U16, "xt_picked")
-        xo_picked = tile([P, J], U32, "xo_picked")
+        xt_picked = tile([P, J], U16, "xt_picked", tag="w_rows")
+        xo_picked = tile([P, J], U32, "xo_picked", tag="xo_picked_rows")
         w_dealt = tile([P, R], I32, "w_dealt")
-        w2_dealt = tile([P, R], I32, "w2_dealt")
+        w2_dealt = tile([P, R], I32, "w2_dealt", tag="xt_picked_rows")
         nc.vector.tensor_copy(xt_picked[:], xt_table[:].indirect(list_t[:]))
         nc.vector.tensor_copy(xo_picked[:], xo_table[:].indirect(list_o[:]))
         for dealt, raw in ((w2_dealt, w2_raw), (w_dealt, w_raw)):
             nc.vector.tensor_copy(
                 dealt[:].rearrange("p (t m) -> p m t", t=PACK), raw[:].rearrange("p (m t) -> p m t", t=PACK)
             )
-
-        sx_sb = tile([P, J], U32, "sx_sb", tag="xo_table")
-        ws_sb = tile([P, N], U32, "ws_sb", tag="w2_raw")
-        wb_sb = tile([P, N], U32, "wb_sb", tag="w_raw")
-        nc.sync.dma_start(out=sx_sb[:].bitcast(I32), in_=words_of(sx_words))
-        nc.sync.dma_start(out=ws_sb[:].bitcast(I32), in_=words_of(ws_words))
-        nc.sync.dma_start(out=wb_sb[:].bitcast(I32), in_=words_of(wb_words))
 
         gate = tile([P, PACK, J], F32, "gate")
         for t in range(PACK):
@@ -171,7 +175,7 @@ def tile_list_crossed_tablegate_skip_scattered_kernel(
             size = [tile([P, RUNS, PACK, RUN], F32, "size%d_%d" % (h, s)) for s in range(PIECES)]
             hid = tile([P, PIECES, RUNS, RUN, PACK], BF16, "hid%d" % h)
             for s in range(PIECES):
-                nc.scalar.copy(out=b_sb[s][:], in_=by_runs(acc_b[h], s * RUNS * RUN))
+                (nc.vector.tensor_copy if h == 0 else nc.scalar.copy)(out=b_sb[s][:], in_=by_runs(acc_b[h], s * RUNS * RUN))
             for s in range(PIECES):
                 nc.vector.tensor_tensor(out=diff[s][:], in0=by_runs(acc_a[h], s * RUNS * RUN), in1=b_sb[s][:], op=ALU.subtract)
                 nc.scalar.activation(out=size[s][:], in_=diff[s][:], func=ACT.Abs)

@@ -90,10 +90,11 @@ def tile_list_crossed_tablegate_skip_scattered_kernel(
         load_scale_rows(nc.sync, late_plane[:, wb_cols], wb_scales)
         load_scale_rows(nc.sync, late_plane[:, sx_cols], sx_scales)
         load_scale_rows(nc.sync, late_plane[:, ws_cols], ws_scales)
+        nc.sync.dma_start(list_g[:], offs3)
         nc.sync.dma_start(out=w2_raw[:], in_=words_of(w2_words))
         nc.sync.dma_start(out=w_raw[:], in_=words_of(w_words))
-        nc.sync.dma_start(list_g[:], offs3)
-        nc.sync.dma_start(out=gates[0][:], in_=tg_dealt[:, 0, :])
+        for t in range(2):
+            nc.sync.dma_start(out=gates[t][:], in_=tg_dealt[:, t, :])
         nc.sync.dma_start(out=slope[:], in_=sg.rearrange("(p t) o -> p (t o)", t=PACK))
 
         warm_in = tile([P, 1], F32, "warm_in")
@@ -115,9 +116,9 @@ def tile_list_crossed_tablegate_skip_scattered_kernel(
         )
         nc.vector.tensor_copy(plane[:, 0:J].bitcast(I32), xt_picked_rows[:].bitcast(I32))
         nc.vector.tensor_copy(plane[:, J : 2 * J].bitcast(I32), xo_picked_rows[:].bitcast(I32))
-        spread_scale_rows(nc.sync, plane)
+        spread_scale_rows(nc.scalar, plane)
         nc.sync.dma_start(out=shift[:], in_=bg.rearrange("(p t) o -> p (t o)", t=PACK))
-        for t in range(1, PACK):
+        for t in range(2, PACK):
             nc.sync.dma_start(out=gates[t][:], in_=tg_dealt[:, t, :])
         nc.sync.dma_start(out=sx_sb[:].bitcast(I32), in_=words_of(sx_words))
         nc.sync.dma_start(out=ws_sb[:].bitcast(I32), in_=words_of(ws_words))

@@ -22,9 +22,6 @@ PACK = 4
 SCALE_ROWS = 16
 HALF = 128
 HALVES = J // HALF
-PIECES = 2
-RUN = 4
-RUNS = HALF // (PIECES * RUN)
 
 
 def words_of(ap):
@@ -67,8 +64,8 @@ def tile_list_crossed_tablegate_skip_scattered_kernel(
 
         xt_table = tile([P, T], U16, "xt_table")
         xo_table = tile([P, T], U32, "xo_table")
-        w_raw = tile([P, R], I32, "w_raw")
-        w2_raw = tile([P, R], I32, "w2_raw")
+        w_raw = tile([P, R], U32, "w_raw")
+        w2_raw = tile([P, R], U32, "w2_raw")
         gates = [tile([P, T], F32, "gates%d" % t) for t in range(PACK)]
         slope = tile([P, PACK], F32, "slope")
         shift = tile([P, PACK], F32, "shift")
@@ -90,11 +87,10 @@ def tile_list_crossed_tablegate_skip_scattered_kernel(
         load_scale_rows(nc.sync, late_plane[:, wb_cols], wb_scales)
         load_scale_rows(nc.sync, late_plane[:, sx_cols], sx_scales)
         load_scale_rows(nc.sync, late_plane[:, ws_cols], ws_scales)
+        nc.sync.dma_start(out=w2_raw[:].bitcast(I32), in_=words_of(w2_words))
+        nc.sync.dma_start(out=w_raw[:].bitcast(I32), in_=words_of(w_words))
         nc.sync.dma_start(list_g[:], offs3)
-        nc.sync.dma_start(out=w2_raw[:], in_=words_of(w2_words))
-        nc.sync.dma_start(out=w_raw[:], in_=words_of(w_words))
-        for t in range(2):
-            nc.sync.dma_start(out=gates[t][:], in_=tg_dealt[:, t, :])
+        nc.sync.dma_start(out=gates[0][:], in_=tg_dealt[:, 0, :])
         nc.sync.dma_start(out=slope[:], in_=sg.rearrange("(p t) o -> p (t o)", t=PACK))
 
         warm_in = tile([P, 1], F32, "warm_in")
@@ -111,14 +107,14 @@ def tile_list_crossed_tablegate_skip_scattered_kernel(
         nc.vector.tensor_copy(xt_picked_rows[:], xt_rows[:].indirect(list_t[:]))
         nc.vector.tensor_copy(xo_picked_rows[:], xo_rows[:].indirect(list_o[:]))
         nc.vector.tensor_copy(
-            plane[:, 2 * J : 2 * J + 2 * R].rearrange("p (w t m) -> p w m t", w=2, t=PACK),
-            w_rows[:].rearrange("p (w m t) -> p w m t", w=2, t=PACK),
+            plane[:, 2 * J : 2 * J + 2 * R].rearrange("p (w t c m) -> p w c t m", w=2, t=PACK, m=16),
+            w_rows[:].rearrange("p (w c m t) -> p w c t m", w=2, t=PACK, m=16),
         )
         nc.vector.tensor_copy(plane[:, 0:J].bitcast(I32), xt_picked_rows[:].bitcast(I32))
         nc.vector.tensor_copy(plane[:, J : 2 * J].bitcast(I32), xo_picked_rows[:].bitcast(I32))
-        spread_scale_rows(nc.scalar, plane)
+        spread_scale_rows(nc.sync, plane)
         nc.sync.dma_start(out=shift[:], in_=bg.rearrange("(p t) o -> p (t o)", t=PACK))
-        for t in range(2, PACK):
+        for t in range(1, PACK):
             nc.sync.dma_start(out=gates[t][:], in_=tg_dealt[:, t, :])
         nc.sync.dma_start(out=sx_sb[:].bitcast(I32), in_=words_of(sx_words))
         nc.sync.dma_start(out=ws_sb[:].bitcast(I32), in_=words_of(ws_words))
@@ -127,13 +123,14 @@ def tile_list_crossed_tablegate_skip_scattered_kernel(
 
         xt_picked = tile([P, J], U16, "xt_picked", tag="w_rows")
         xo_picked = tile([P, J], U32, "xo_picked", tag="xo_picked_rows")
-        w_dealt = tile([P, R], I32, "w_dealt")
-        w2_dealt = tile([P, R], I32, "w2_dealt", tag="xt_picked_rows")
+        w_dealt = tile([P, R], U32, "w_dealt")
+        w2_dealt = tile([P, R], U32, "w2_dealt")
         nc.vector.tensor_copy(xt_picked[:], xt_table[:].indirect(list_t[:]))
         nc.vector.tensor_copy(xo_picked[:], xo_table[:].indirect(list_o[:]))
         for dealt, raw in ((w2_dealt, w2_raw), (w_dealt, w_raw)):
-            nc.vector.tensor_copy(
-                dealt[:].rearrange("p (t m) -> p m t", t=PACK), raw[:].rearrange("p (m t) -> p m t", t=PACK)
+            nc.scalar.copy(
+                out=dealt[:].rearrange("p (t c m) -> p c t m", t=PACK, m=4),
+                in_=raw[:].rearrange("p (c m t) -> p c t m", t=PACK, m=4),
             )
 
         gate = tile([P, PACK, J], F32, "gate")
@@ -143,14 +140,18 @@ def tile_list_crossed_tablegate_skip_scattered_kernel(
                 bias=shift[:, t : t + 1], scale=slope[:, t : t + 1],
             )
 
+        w_side = (w_dealt, E5M2, 2 * J)
+        w2_side = (w2_dealt, E4M3, 2 * J + R)
+
+        halves = [slice(h * HALF, (h + 1) * HALF) for h in range(HALVES)]
+
         def first_stage(acc, h, with_xt, with_xo):
-            cols = slice(h * HALF, (h + 1) * HALF)
-            moving = (
-                (with_xt, xt_picked[:, cols].bitcast(E2M1), plane[:, h * HALF : (h + 1) * HALF]),
-                (with_xo, xo_picked[:, cols].bitcast(E5M2), plane[:, J + h * HALF : J + (h + 1) * HALF]),
+            passes = (
+                (with_xt, xt_picked[:, halves[h]].bitcast(E2M1), plane[:, h * HALF : (h + 1) * HALF]),
+                (with_xo, xo_picked[:, halves[h]].bitcast(E5M2), plane[:, J + h * HALF : J + (h + 1) * HALF]),
             )
             for t in range(PACK):
-                for n, ((dealt, fmt, first_col), rhs, rhs_scale) in enumerate(moving):
+                for n, ((dealt, fmt, first_col), rhs, rhs_scale) in enumerate(passes):
                     nc.tensor.matmul_mx(
                         out=acc[:, t, :],
                         lhsT=dealt[:, t * P : (t + 1) * P].bitcast(fmt),
@@ -158,60 +159,54 @@ def tile_list_crossed_tablegate_skip_scattered_kernel(
                         rhs=rhs, rhs_scale=rhs_scale, start=(n == 0), stop=(n == 1),
                     )
 
-        w_side = (w_dealt, E5M2, 2 * J)
-        w2_side = (w2_dealt, E4M3, 2 * J + R)
-        acc_a = [psum.tile([P, PACK, HALF], F32, name="acc_a%d" % h, tag="bank_a%d" % h) for h in range(HALVES)]
-        acc_b = [psum.tile([P, PACK, HALF], F32, name="acc_b%d" % h, tag="bank_b%d" % h) for h in range(HALVES)]
+        gated = [tile([P, PACK, HALF], F32, "gated%d" % h) for h in range(HALVES)]
         for h in range(HALVES):
-            first_stage(acc_b[h], h, w2_side, w_side)
-            first_stage(acc_a[h], h, w_side, w2_side)
+            acc_b = psum.tile([P, PACK, HALF], F32, name="acc_b%d" % h, tag="bank%d" % (2 * h))
+            acc_a = psum.tile([P, PACK, HALF], F32, name="acc_a%d" % h, tag="bank%d" % (2 * h + 1))
+            first_stage(acc_b, h, w2_side, w_side)
+            first_stage(acc_a, h, w_side, w2_side)
+            b_sb = tile([P, PACK, HALF], F32, "b_sb%d" % h)
+            diff = tile([P, PACK, HALF], F32, "diff%d" % h)
+            nc.vector.tensor_copy(out=b_sb[:], in_=acc_b[:])
+            nc.vector.tensor_tensor(out=diff[:], in0=acc_a[:], in1=b_sb[:], op=ALU.subtract)
+            nc.vector.tensor_tensor(out=gated[h][:], in0=diff[:], in1=gate[:, :, halves[h]], op=ALU.mult)
 
-
-        def by_runs(ap, first):
-            return ap[:, :, first : first + RUNS * RUN].rearrange("p t (c i) -> p c t i", i=RUN)
-
+        acc_p = [
+            [psum.tile([P, HALF], F32, name="acc_p%d_%d" % (h, nt), tag="bank%d" % (2 * h + nt)) for nt in range(N // P)]
+            for h in range(HALVES)
+        ]
         for h in range(HALVES):
-            b_sb = [tile([P, RUNS, PACK, RUN], F32, "b_sb%d_%d" % (h, s)) for s in range(PIECES)]
-            diff = [tile([P, RUNS, PACK, RUN], F32, "diff%d_%d" % (h, s)) for s in range(PIECES)]
-            size = [tile([P, RUNS, PACK, RUN], F32, "size%d_%d" % (h, s)) for s in range(PIECES)]
-            hid = tile([P, PIECES, RUNS, RUN, PACK], BF16, "hid%d" % h)
-            for s in range(PIECES):
-                (nc.vector.tensor_copy if h == 0 else nc.scalar.copy)(out=b_sb[s][:], in_=by_runs(acc_b[h], s * RUNS * RUN))
-            for s in range(PIECES):
-                nc.vector.tensor_tensor(out=diff[s][:], in0=by_runs(acc_a[h], s * RUNS * RUN), in1=b_sb[s][:], op=ALU.subtract)
-                nc.scalar.activation(out=size[s][:], in_=diff[s][:], func=ACT.Abs)
-            acc_p = [psum.tile([P, HALF], F32, name="acc_p%d_%d" % (h, nt), tag="bank_%s%d" % (side, h)) for nt, side in enumerate("ba")]
             for nt in range(N // P):
                 nc.tensor.matmul_mx(
-                    out=acc_p[nt][:],
+                    out=acc_p[h][nt][:],
                     lhsT=ws_sb[:, nt * P : (nt + 1) * P].bitcast(E4M3),
                     lhsT_scale=late_plane[:, N + J + nt * P : N + J + (nt + 1) * P],
-                    rhs=sx_sb[:, h * HALF : (h + 1) * HALF].bitcast(E5M2),
+                    rhs=sx_sb[:, halves[h]].bitcast(E5M2),
                     rhs_scale=late_plane[:, N + h * HALF : N + (h + 1) * HALF],
                     start=True, stop=False,
                 )
-            for s in range(PIECES):
-                nc.vector.tensor_tensor(
-                    out=hid[:, s].rearrange("p c i t -> p c t i"), in0=size[s][:],
-                    in1=by_runs(gate, h * HALF + s * RUNS * RUN), op=ALU.mult,
-                )
-            hid_words = tile([P, HALF], U32, "hid_words%d" % h)
-            hid_plane = tile([P, HALF], U8, "hid_plane%d" % h)
+
+        hid = [tile([P, HALF, PACK], BF16, "hid%d" % h) for h in range(HALVES)]
+        hid_words = [tile([P, HALF], U32, "hid_words%d" % h) for h in range(HALVES)]
+        hid_plane = [tile([P, HALF], U8, "hid_plane%d" % h) for h in range(HALVES)]
+        for h in range(HALVES):
+            nc.scalar.activation(out=hid[h][:], in_=gated[h][:].rearrange("p t j -> p j t"), func=ACT.Abs)
             nc.vector.quantize_mx(
-                out=hid_words[:].bitcast(E5M2), scales=hid_plane[:], in_=hid[:].rearrange("p s c i t -> p (s c i t)")
+                out=hid_words[h][:].bitcast(E5M2), scales=hid_plane[h][:], in_=hid[h][:].rearrange("p j t -> p (j t)")
             )
-            places = list_p[:, h * HALF // 16 : (h + 1) * HALF // 16]
             for nt in range(N // P):
                 nc.tensor.matmul_mx(
-                    out=acc_p[nt][:],
+                    out=acc_p[h][nt][:],
                     lhsT=wb_sb[:, nt * P : (nt + 1) * P].bitcast(E4M3),
                     lhsT_scale=late_plane[:, nt * P : (nt + 1) * P],
-                    rhs=hid_words[:].bitcast(E5M2), rhs_scale=hid_plane[:],
+                    rhs=hid_words[h][:].bitcast(E5M2), rhs_scale=hid_plane[h][:],
                     start=False, stop=True,
                 )
-            p_sb = [tile([P, HALF], F32, "p_sb%d_%d" % (h, nt)) for nt in range(N // P)]
-            nc.vector.tensor_copy(p_sb[0][:], acc_p[0][:])
-            nc.scalar.copy(out=p_sb[1][:], in_=acc_p[1][:])
+        for h in range(HALVES):
+            places = list_p[:, h * HALF // 16 : (h + 1) * HALF // 16]
+            p_sb = [tile([P, HALF], F32, "p_sb%d_%d" % (h, nt), tag="hid%d" % (1 - nt) if h == 0 else None) for nt in range(N // P)]
+            nc.vector.tensor_copy(p_sb[0][:], acc_p[h][0][:])
+            nc.scalar.copy(out=p_sb[1][:], in_=acc_p[h][1][:])
             nc.vector.tensor_copy(pages[0][:].indirect(places), p_sb[0][:])
             nc.scalar.activation(out=pages[1][:].indirect(places), in_=p_sb[1][:], func=ACT.Copy)
 

from contextlib import ExitStack

import concourse.mybir as mybir

K, T, J, R, N, E = 512, 1024, 256, 512, 256, 1024
FLOPS = 2 * (4 * K * R * J + R * N * J + K * N * J)

F32 = mybir.dt.float32
BF16 = mybir.dt.bfloat16
I32 = mybir.dt.int32
U32 = mybir.dt.uint32
U16 = mybir.dt.uint16
U8 = mybir.dt.uint8
E4M3 = mybir.dt.float8_e4m3fn_x4
E5M2 = mybir.dt.float8_e5m2_x4
E2M1 = mybir.dt.float4_e2m1fn_x4
ACT = mybir.ActivationFunctionType
ALU = mybir.AluOpType

P = 128
PACK = 4
SCALE_ROWS = 16
HALF = 128
HALVES = J // HALF


def words_of(ap):
    return ap[0].rearrange("p c b -> p (c b)").bitcast(I32)


def tile_list_crossed_tablegate_skip_scattered_kernel(
    tc, xt_words, xt_scales, xo_words, xo_scales, w_words, w_scales, w2_words, w2_scales, tg, sg, bg,
    wb_words, wb_scales, sx_words, sx_scales, ws_words, ws_scales, offs, offs2, offs3, offs4, out,
):
    nc = tc.nc
    with ExitStack() as ctx:
        pool = ctx.enter_context(tc.tile_pool(name="pool", bufs=1))
        psum = ctx.enter_context(tc.psum_pool(name="psum", bufs=1))

        def tile(shape, dtype, name, tag=None):
            return pool.tile(shape, dtype, name=name, tag=tag or name, align_bytes=64)

        def load_scale_rows(queue, dst, src):
            queue.dma_start(out=dst[0:SCALE_ROWS, :].bitcast(I32), in_=src[0].bitcast(I32))

        def spread_scale_rows(queue, plane):
            for q in range(1, 4):
                queue.dma_start(out=plane[32 * q : 32 * q + 4, :].bitcast(I32), in_=plane[4 * q : 4 * q + 4, :].bitcast(I32))

        list_t = tile([P, J // 16], U16, "list_t")
        list_o = tile([P, J // 16], U16, "list_o")
        list_g = tile([P, J // 16], U16, "list_g")
        list_p = tile([P, J // 16], U16, "list_p")

        xt_rows = tile([P, T], U8, "xt_rows")
        xo_rows = tile([P, T], U8, "xo_rows")
        w_rows = tile([P, 2 * R], U8, "w_rows")
        plane = tile([P, 2 * J + 2 * R + 2 * N + J], U8, "plane")
        late_plane = plane[:, 2 * J + 2 * R :]
        nc.gpsimd.memset(xt_rows[:].bitcast(I32), 0)
        nc.gpsimd.memset(xo_rows[:].bitcast(I32), 0)
        nc.vector.memset(w_rows[:].bitcast(I32), 0)
        nc.vector.memset(late_plane.bitcast(I32), 0)

        xt_table = tile([P, T], U16, "xt_table")
        xo_table = tile([P, T], U32, "xo_table")
        w_raw = tile([P, R], U32, "w_raw")
        w2_raw = tile([P, R], U32, "w2_raw")
        gates = [tile([P, T], F32, "gates%d" % t) for t in range(PACK)]
        slope = tile([P, PACK], F32, "slope")
        shift = tile([P, PACK], F32, "shift")

        wb_sb = tile([P, N], U32, "wb_sb")
        sx_sb = tile([P, J], U32, "sx_sb")
        ws_sb = tile([P, N], U32, "ws_sb")
        wb_cols, sx_cols, ws_cols = slice(0, N), slice(N, N + J), slice(N + J, 2 * N + J)
        tg_dealt = tg.rearrange("(p t) q -> p t q", t=PACK)

        nc.sync.dma_start(list_t[:], offs)
        nc.sync.dma_start(list_o[:], offs2)
        load_scale_rows(nc.sync, xt_rows, xt_scales)
        load_scale_rows(nc.sync, xo_rows, xo_scales)
        load_scale_rows(nc.scalar, w_rows[:, 0:R], w_scales)
        load_scale_rows(nc.scalar, w_rows[:, R : 2 * R], w2_scales)
        nc.sync.dma_start(out=xt_table[:].bitcast(I32), in_=xt_words[0].bitcast(I32))
        nc.sync.dma_start(out=xo_table[:].bitcast(I32), in_=words_of(xo_words))
        load_scale_rows(nc.sync, late_plane[:, wb_cols], wb_scales)
        load_scale_rows(nc.sync, late_plane[:, sx_cols], sx_scales)
        load_scale_rows(nc.sync, late_plane[:, ws_cols], ws_scales)
        nc.sync.dma_start(out=w2_raw[:].bitcast(I32), in_=words_of(w2_words))
        nc.sync.dma_start(out=w_raw[:].bitcast(I32), in_=words_of(w_words))
        nc.sync.dma_start(list_g[:], offs3)
        nc.sync.dma_start(out=gates[0][:], in_=tg_dealt[:, 0, :])
        nc.sync.dma_start(out=slope[:], in_=sg.rearrange("(p t) o -> p (t o)", t=PACK))

        warm_in = tile([P, 1], F32, "warm_in")
        warm_out = tile([P, 1], F32, "warm_out")
        nc.gpsimd.memset(warm_in[:], 0.0)
        nc.scalar.activation(out=warm_out[:], in_=warm_in[:], func=ACT.Sigmoid)

        pages = [tile([P, E], F32, "page%d" % nt) for nt in range(N // P)]
        nc.vector.memset(pages[0][:], 0.0)
        nc.gpsimd.memset(pages[1][:], 0.0)

        xt_picked_rows = tile([P, J], U8, "xt_picked_rows")
        xo_picked_rows = tile([P, J], U8, "xo_picked_rows")
        nc.vector.tensor_copy(xt_picked_rows[:], xt_rows[:].indirect(list_t[:]))
        nc.vector.tensor_copy(xo_picked_rows[:], xo_rows[:].indirect(list_o[:]))
        nc.vector.tensor_copy(
            plane[:, 2 * J : 2 * J + 2 * R].rearrange("p (w t c m) -> p w c t m", w=2, t=PACK, m=16),
            w_rows[:].rearrange("p (w c m t) -> p w c t m", w=2, t=PACK, m=16),
        )
        nc.vector.tensor_copy(plane[:, 0:J].bitcast(I32), xt_picked_rows[:].bitcast(I32))
        nc.vector.tensor_copy(plane[:, J : 2 * J].bitcast(I32), xo_picked_rows[:].bitcast(I32))
        spread_scale_rows(nc.sync, plane)
        nc.sync.dma_start(out=shift[:], in_=bg.rearrange("(p t) o -> p (t o)", t=PACK))
        for t in range(1, PACK):
            nc.sync.dma_start(out=gates[t][:], in_=tg_dealt[:, t, :])
        nc.sync.dma_start(out=sx_sb[:].bitcast(I32), in_=words_of(sx_words))
        nc.sync.dma_start(out=ws_sb[:].bitcast(I32), in_=words_of(ws_words))
        nc.sync.dma_start(out=wb_sb[:].bitcast(I32), in_=words_of(wb_words))
        nc.sync.dma_start(list_p[:], offs4)

        xt_picked = tile([P, J], U16, "xt_picked", tag="w_rows")
        xo_picked = tile([P, J], U32, "xo_picked", tag="xo_picked_rows")
        w_dealt = tile([P, R], U32, "w_dealt")
        w2_dealt = tile([P, R], U32, "w2_dealt")
        nc.vector.tensor_copy(xt_picked[:], xt_table[:].indirect(list_t[:]))
        nc.vector.tensor_copy(xo_picked[:], xo_table[:].indirect(list_o[:]))
        for dealt, raw in ((w2_dealt, w2_raw), (w_dealt, w_raw)):
            nc.scalar.copy(
                out=dealt[:].rearrange("p (t c m) -> p c t m", t=PACK, m=4),
                in_=raw[:].rearrange("p (c m t) -> p c t m", t=PACK, m=4),
            )

        gate = tile([P, PACK, J], F32, "gate")
        for t in range(PACK):
            nc.scalar.activation(
                out=gate[:, t, :], in_=gates[t][:].indirect(list_g[:]), func=ACT.Sigmoid,
                bias=shift[:, t : t + 1], scale=slope[:, t : t + 1],
            )

        w_side = (w_dealt, E5M2, 2 * J)
        w2_side = (w2_dealt, E4M3, 2 * J + R)

        halves = [slice(h * HALF, (h + 1) * HALF) for h in range(HALVES)]

        def first_stage(acc, h, with_xt, with_xo):
            passes = (
                (with_xt, xt_picked[:, halves[h]].bitcast(E2M1), plane[:, h * HALF : (h + 1) * HALF]),
                (with_xo, xo_picked[:, halves[h]].bitcast(E5M2), plane[:, J + h * HALF : J + (h + 1) * HALF]),
            )
            for t in range(PACK):
                for n, ((dealt, fmt, first_col), rhs, rhs_scale) in enumerate(passes):
                    nc.tensor.matmul_mx(
                        out=acc[:, t, :],
                        lhsT=dealt[:, t * P : (t + 1) * P].bitcast(fmt),
                        lhsT_scale=plane[:, first_col + t * P : first_col + (t + 1) * P],
                        rhs=rhs, rhs_scale=rhs_scale, start=(n == 0), stop=(n == 1),
                    )

        gated = [tile([P, PACK, HALF], F32, "gated%d" % h) for h in range(HALVES)]
        for h in range(HALVES):
            acc_b = psum.tile([P, PACK, HALF], F32, name="acc_b%d" % h, tag="bank%d" % (2 * h))
            acc_a = psum.tile([P, PACK, HALF], F32, name="acc_a%d" % h, tag="bank%d" % (2 * h + 1))
            first_stage(acc_b, h, w2_side, w_side)
            first_stage(acc_a, h, w_side, w2_side)
            b_sb = tile([P, PACK, HALF], F32, "b_sb%d" % h)
            diff = tile([P, PACK, HALF], F32, "diff%d" % h)
            nc.vector.tensor_copy(out=b_sb[:], in_=acc_b[:])
            nc.vector.tensor_tensor(out=diff[:], in0=acc_a[:], in1=b_sb[:], op=ALU.subtract)
            nc.vector.tensor_tensor(out=gated[h][:], in0=diff[:], in1=gate[:, :, halves[h]], op=ALU.mult)

        acc_p = [
            [psum.tile([P, HALF], F32, name="acc_p%d_%d" % (h, nt), tag="bank%d" % (2 * h + nt)) for nt in range(N // P)]
            for h in range(HALVES)
        ]
        for h in range(HALVES):
            for nt in range(N // P):
                nc.tensor.matmul_mx(
                    out=acc_p[h][nt][:],
                    lhsT=ws_sb[:, nt * P : (nt + 1) * P].bitcast(E4M3),
                    lhsT_scale=late_plane[:, N + J + nt * P : N + J + (nt + 1) * P],
                    rhs=sx_sb[:, halves[h]].bitcast(E5M2),
                    rhs_scale=late_plane[:, N + h * HALF : N + (h + 1) * HALF],
                    start=True, stop=False,
                )

        hid = [tile([P, HALF, PACK], BF16, "hid%d" % h) for h in range(HALVES)]
        hid_words = [tile([P, HALF], U32, "hid_words%d" % h) for h in range(HALVES)]
        hid_plane = [tile([P, HALF], U8, "hid_plane%d" % h) for h in range(HALVES)]
        for h in range(HALVES):
            nc.scalar.activation(out=hid[h][:], in_=gated[h][:].rearrange("p t j -> p j t"), func=ACT.Abs)
            nc.vector.quantize_mx(
                out=hid_words[h][:].bitcast(E5M2), scales=hid_plane[h][:], in_=hid[h][:].rearrange("p j t -> p (j t)")
            )
            for nt in range(N // P):
                nc.tensor.matmul_mx(
                    out=acc_p[h][nt][:],
                    lhsT=wb_sb[:, nt * P : (nt + 1) * P].bitcast(E4M3),
                    lhsT_scale=late_plane[:, nt * P : (nt + 1) * P],
                    rhs=hid_words[h][:].bitcast(E5M2), rhs_scale=hid_plane[h][:],
                    start=False, stop=True,
                )
        for h in range(HALVES):
            places = list_p[:, h * HALF // 16 : (h + 1) * HALF // 16]
            p_sb = [tile([P, HALF], F32, "p_sb%d_%d" % (h, nt), tag="hid%d" % (1 - nt) if h == 0 else None) for nt in range(N // P)]
            nc.vector.tensor_copy(p_sb[0][:], acc_p[h][0][:])
            nc.scalar.copy(out=p_sb[1][:], in_=acc_p[h][1][:])
            nc.vector.tensor_copy(pages[0][:].indirect(places), p_sb[0][:])
            nc.scalar.activation(out=pages[1][:].indirect(places), in_=p_sb[1][:], func=ACT.Copy)

        nc.sync.dma_start(out=out[0:P, :], in_=pages[0][:])
        nc.scalar.dma_start(out=out[P : 2 * P, :], in_=pages[1][:])
